import numpy as np
import ml_dtypes


def mxq(x, axis, fmt="e4m3"):
    dtype, down = {"e4m3": (ml_dtypes.float8_e4m3fn, 7), "e5m2": (ml_dtypes.float8_e5m2, 14)}[fmt]
    v = np.moveaxis(np.asarray(x, np.float32).astype(ml_dtypes.bfloat16).astype(np.float64), axis, -1)
    blocks = v.reshape(v.shape[:-1] + (-1, 32))
    amax = np.abs(blocks).max(-1, keepdims=True)
    byte = np.maximum(np.where(amax > 0, np.frexp(amax)[1] - 1 + 127, 0) - down, 1)
    scale = np.exp2(byte - 127.0)
    codes = (blocks / scale).astype(np.float32).astype(dtype).astype(np.float64)
    return np.moveaxis((codes * scale).reshape(v.shape), -1, axis)


WIDE = False


def mx_kscale(k):
    if not WIDE:
        return np.ones(k)
    levels = np.array([30, -30])
    if k % 512:
        return np.exp2(np.random.permutation(np.resize(levels, k // 32))).repeat(32)
    a = np.empty((k // 512, 16))
    for p in range(k // 512):
        a[p, :8] = np.random.permutation(np.resize(levels, 8))
        for g in range(8):
            far = levels[np.abs(levels - a[p, g]) >= 10]
            a[p, g + 8] = far[np.random.randint(len(far))]
    return np.exp2(a.ravel()).repeat(32)


def f64(x):
    return np.asarray(x).astype(np.float64)


def striped(idx):
    return np.tile(np.asarray(idx).reshape(-1, 16).T, (8, 1)).astype(np.uint16)


def unstriped(offs):
    return offs[:16].T.reshape(-1).astype(np.int64)


def striped8(idx):
    return np.asarray(idx).reshape(8, -1, 16).transpose(0, 2, 1).reshape(128, -1).astype(np.uint16)


def unstriped8(offs):
    return offs.reshape(8, 16, -1).transpose(0, 2, 1).reshape(8, -1).astype(np.int64)


def pick8(x, idx, run):
    r = np.arange(len(x))
    return x[r[:, None], idx[r % (8 * run) // run]]


E2M1 = np.array([0.0, 0.5, 1.0, 1.5, 2.0, 3.0, 4.0, 6.0, -0.0, -0.5, -1.0, -1.5, -2.0, -3.0, -4.0, -6.0])


def pack_weight(w, fmt):
    k, n = w.shape
    w = f64(np.asarray(w, np.float32).astype(ml_dtypes.bfloat16)).reshape(k // 32, 32, n)
    amax = np.abs(w).max(1)
    if fmt in ("e4m3", "e5m2"):
        byte = np.frexp(amax)[1] - 1 + 127 - (7 if fmt == "e4m3" else 14)
    else:
        mant, ex = np.frexp(amax / 6.0)
        byte = np.where(mant > 0.5, ex, ex - 1) + 127
    byte = np.clip(np.where(amax > 0, byte, 1), 1, 254)
    scaled = (w * np.exp2(127.0 - byte)[:, None, :]).reshape(k, n).astype(np.float32)
    by_word = np.ascontiguousarray(scaled.reshape(k // 512, 128, 4, n).transpose(0, 1, 3, 2))
    if fmt in ("e4m3", "e5m2"):
        words = by_word.astype(ml_dtypes.float8_e4m3fn if fmt == "e4m3" else ml_dtypes.float8_e5m2).view(np.uint8)
    else:
        c = by_word.astype(ml_dtypes.float4_e2m1fn).view(np.uint8) & 0xF
        words = (c[..., 0::2] | (c[..., 1::2] << 4)).reshape(k // 512, 128, 2 * n)
    return np.ascontiguousarray(words), np.ascontiguousarray(byte.astype(np.uint8).reshape(k // 512, 16, n))


def unpack_weight(words, scales, fmt):
    g, _, n = scales.shape
    words = np.ascontiguousarray(words).reshape(g, 128, n, -1)
    if fmt in ("e4m3", "e5m2"):
        vals = words.view(ml_dtypes.float8_e4m3fn if fmt == "e4m3" else ml_dtypes.float8_e5m2).astype(np.float64)
    else:
        nib = np.empty((g, 128, n, 4), np.uint8)
        nib[..., 0::2] = words & 0xF
        nib[..., 1::2] = words >> 4
        vals = E2M1[nib]
    vals = vals * np.repeat(np.exp2(scales.astype(np.float64) - 127.0), 8, axis=1)[..., None]
    return vals.transpose(0, 1, 3, 2).reshape(g * 512, n)


K, T, J, R, C, D, O, N, S, E = 512, 1024, 256, 512, 512, 512, 128, 256, 1024, 1024


def setup_inputs():
    n = np.random.standard_normal
    idx = np.random.permutation(T)[:J]
    idx2 = np.stack([np.random.permutation(C)[:J] for _ in range(8)])
    idx3 = np.random.permutation(D)[:J]
    idx4 = np.random.permutation(C)[:O]
    idx5 = np.stack([np.random.permutation(D)[:O] for _ in range(8)])
    idx6 = np.random.permutation(S)[:N]
    idx7 = np.random.permutation(E)[:O]
    fk = mx_kscale(K)
    fr = mx_kscale(R)
    xtp = pack_weight(n((K, T)) / fk[:, None], "e5m2")
    wp = pack_weight(n((K, R)) * 1 / np.sqrt(K) * fk[:, None] * fr, "e2m1")
    w2p = pack_weight(n((K, R)) * 1 / np.sqrt(K) * fk[:, None] * fr, "e4m3")
    vsp = pack_weight(n((R, S)) * 1 / np.sqrt(R) / fr[:, None], "e2m1")
    return {
        "xt_words": xtp[0],
        "xt_scales": xtp[1],
        "w_words": wp[0],
        "w_scales": wp[1],
        "w2_words": w2p[0],
        "w2_scales": w2p[1],
        "sa": (np.random.uniform(0.5, 1.6, (R, 1))).astype(np.float32),
        "sb": (np.random.uniform(0.5, 1.6, (R, 1))).astype(np.float32),
        "vs_words": vsp[0],
        "vs_scales": vsp[1],
        "offs": striped(idx),
        "offs2": striped8(idx2),
        "offs3": striped(idx3),
        "offs4": striped(idx4),
        "offs5": striped8(idx5),
        "offs6": striped(idx6),
        "offs7": striped(idx7),
    }


def reference(xt_words, xt_scales, w_words, w_scales, w2_words, w2_scales, sa, sb, vs_words, vs_scales, offs, offs2, offs3, offs4, offs5, offs6, offs7):
    idx = unstriped(offs)
    idx2 = unstriped8(offs2)
    idx3 = unstriped(offs3)
    idx4 = unstriped(offs4)
    idx5 = unstriped8(offs5)
    idx6 = unstriped(offs6)
    idx7 = unstriped(offs7)
    xtu = unpack_weight(xt_words, xt_scales, "e5m2")
    wu = unpack_weight(w_words, w_scales, "e2m1")
    w2u = unpack_weight(w2_words, w2_scales, "e4m3")
    vsu = unpack_weight(vs_words, vs_scales, "e2m1")
    xtidxg = xtu[:, idx]
    a = wu.T @ xtidxg
    b = w2u.T @ xtidxg
    pw = np.zeros((R, C))
    pw[np.arange(R)[:, None], idx2[np.arange(R) % 512 // 64]] = a
    pv = np.zeros((R, D))
    pv[:, idx3] = b
    hid = np.abs(pw[:, idx4] * f64(sa) - pick8(pv, idx5, 64) * f64(sb))
    vsidx6g = vsu[:, idx6]
    hidq = mxq(hid, 0, "e4m3")
    p = vsidx6g.T @ hidq
    y = np.zeros((N, E))
    y[:, idx7] = p
    return y

@@ -1,0 +1,202 @@
+from contextlib import ExitStack
+
+import concourse.mybir as mybir
+
+K, T, J, R, C, D, O, N, S, E = 512, 1024, 256, 512, 512, 512, 128, 256, 1024, 1024
+FLOPS = 2 * K * R * J * 2 + 2 * R * N * O
+
+F32 = mybir.dt.float32
+BF16 = mybir.dt.bfloat16
+I32 = mybir.dt.int32
+U32 = mybir.dt.uint32
+U16 = mybir.dt.uint16
+U8 = mybir.dt.uint8
+E4M3X4 = mybir.dt.float8_e4m3fn_x4
+E5M2X4 = mybir.dt.float8_e5m2_x4
+E2M1X4 = mybir.dt.float4_e2m1fn_x4
+ACT = mybir.ActivationFunctionType
+ALU = mybir.AluOpType
+
+P = 128
+PACK = 4
+QUADS = 4
+QUAD = 32
+
+
+def tile_list_owncommon_twow_store_scattered_kernel(
+    tc, xt_words, xt_scales, w_words, w_scales, w2_words, w2_scales, sa, sb, vs_words, vs_scales,
+    offs, offs2, offs3, offs4, offs5, offs6, offs7, out,
+):
+    nc = tc.nc
+    with ExitStack() as ctx:
+        keep = ctx.enter_context(tc.tile_pool(name="keep", bufs=1))
+        psum = ctx.enter_context(tc.psum_pool(name="psum", bufs=1))
+
+        def load_list(name, src):
+            tile = keep.tile(list(src.shape), U16, name=name)
+            nc.sync.dma_start(tile[:], src)
+            return tile
+
+        def load_scale_plane(name, scales, width):
+            window = keep.tile([P, width], U8, name=name, align_bytes=64)
+            nc.vector.memset(window[:].bitcast(I32), 0)
+            for r in range(PACK):
+                nc.sync.dma_start(window[r:P:QUAD, :].bitcast(I32), scales[0, r : QUADS * PACK : PACK, :].bitcast(I32))
+            return window
+
+        def load_scale_rows(name, scales):
+            rows = keep.tile([PACK, QUADS, R], U8, name=name, align_bytes=64)
+            nc.sync.dma_start(rows[:].bitcast(I32), scales[0].rearrange("(q r) n -> r q n", r=PACK).bitcast(I32))
+            return rows
+
+        def spread_scales(name, rows):
+            spread = keep.tile([P, R], U8, name=name + "_spread", align_bytes=64)
+            nc.vector.memset(spread[:].bitcast(I32), 0)
+            for q in range(QUADS):
+                nc.vector.tensor_copy(spread[QUAD * q : QUAD * q + PACK, :].bitcast(I32), rows[:, q, :].bitcast(I32))
+            return spread
+
+        def deal_scales(name, spread):
+            dealt = keep.tile([P, R], U8, name=name + "_dealt", align_bytes=64)
+            nc.vector.tensor_copy(
+                dealt[:].rearrange("p (t m) -> p m t", t=PACK), spread[:].rearrange("p (m t) -> p m t", t=PACK)
+            )
+            return dealt
+
+        ws_rows = load_scale_rows("ws_rows", w_scales)
+        idx = load_list("idx", offs)
+        xs_win = load_scale_plane("xs_win", xt_scales, T)
+        w_raw = keep.tile([P, R], U16, name="w_raw", align_bytes=64)
+        nc.sync.dma_start(w_raw[:].bitcast(I32), w_words[0].bitcast(I32))
+        xt_win = keep.tile([P, T], U32, name="xt_win", tag="page0", align_bytes=64)
+        nc.sync.dma_start(xt_win[:].bitcast(I32), xt_words[0].rearrange("p n t -> p (n t)").bitcast(I32))
+        w2s_plane = load_scale_plane("w2s_plane", w2_scales, R)
+        w2_raw = keep.tile([P, R], U32, name="w2_raw", tag="page1", align_bytes=64)
+        nc.sync.dma_start(w2_raw[:].bitcast(I32), w2_words[0].rearrange("p n t -> p (n t)").bitcast(I32))
+        idx2 = load_list("idx2", offs2)
+        idx3 = load_list("idx3", offs3)
+        idx4 = load_list("idx4", offs4)
+        sa_t = keep.tile([P, PACK], F32, name="sa_t")
+        nc.sync.dma_start(sa_t[:], sa.rearrange("(p t) o -> p (t o)", t=PACK))
+        idx5 = load_list("idx5", offs5)
+        sb_t = keep.tile([P, PACK], F32, name="sb_t")
+        nc.sync.dma_start(sb_t[:], sb.rearrange("(p t) o -> p (t o)", t=PACK))
+
+        ws = deal_scales("ws", spread_scales("ws", ws_rows))
+        wd = keep.tile([P, R], U16, name="wd", align_bytes=64)
+        nc.scalar.copy(wd[:].rearrange("p (t m) -> p m t", t=PACK), w_raw[:].rearrange("p (m t) -> p m t", t=PACK))
+        xs_g = keep.tile([P, J], U8, name="xs_g", align_bytes=64)
+        nc.vector.tensor_copy(xs_g[:], xs_win[:].indirect(idx[:]))
+        x_g = keep.tile([P, J], U32, name="x_g", align_bytes=64)
+        nc.vector.tensor_copy(x_g[:], xt_win[:].indirect(idx[:]))
+        w2s = deal_scales("w2s", w2s_plane)
+        w2d = keep.tile([P, R], U32, name="w2d", align_bytes=64)
+        nc.vector.tensor_copy(
+            w2d[:].bitcast(I32).rearrange("p (t m) -> p m t", t=PACK),
+            w2_raw[:].bitcast(I32).rearrange("p (m t) -> p m t", t=PACK),
+        )
+
+        pw = [keep.tile([P, C], F32, name="pw%d" % i) for i in range(2)]
+        pv = [keep.tile([P, D], F32, name="pv%d" % i) for i in range(3)]
+        for board in pw + pv:
+            nc.vector.memset(board[:], 0.0)
+
+        vs_win = keep.tile([P, S], U16, name="vs_win", align_bytes=64)
+        nc.sync.dma_start(vs_win[:].bitcast(I32), vs_words[0].bitcast(I32))
+        idx6 = load_list("idx6", offs6)
+        vss_win = load_scale_plane("vss_win", vs_scales, S)
+        idx7 = load_list("idx7", offs7)
+
+        def product(name, words, scales, dtype, t):
+            acc = psum.tile([P, J], F32, name="%s%d" % (name, t), tag="%s%d" % (name, t))
+            cols = slice(t * P, (t + 1) * P)
+            nc.tensor.matmul_mx(
+                out=acc[:], lhsT=words[:, cols].bitcast(dtype), lhsT_scale=scales[:, cols],
+                rhs=x_g[:].bitcast(E5M2X4), rhs_scale=xs_g[:], start=True, stop=True,
+            )
+            return acc
+
+        a_ps = [product("a", wd, ws, E2M1X4, t) for t in range(PACK)]
+        b_ps = [product("b", w2d, w2s, E4M3X4, t) for t in range(PACK)]
+
+        pages = []
+        for h in range(N // P):
+            page = keep.tile([P, E], F32, name="page%d" % h, tag="page%d" % h, align_bytes=64)
+            for half in range(2):
+                nc.gpsimd.memset(page[:, half * (E // 2) : (half + 1) * (E // 2)], 0.0)
+            pages.append(page)
+
+        a_sb = [keep.tile([P, J], F32, name="a_sb%d" % t, tag="a_sb%d" % t, align_bytes=64) for t in range(PACK)]
+        us, vs = [], []
+
+        def scatter_a(t):
+            if t < 2:
+                nc.scalar.copy(a_sb[t][:], a_ps[t][:])
+            nc.scalar.activation(pw[t % 2][:].indirect(idx2[:]), a_sb[t][:], ACT.Copy)
+
+        def scatter_b(t):
+            b_sb = keep.tile([P, J], F32, name="b_sb%d" % t, tag="b_sb%d" % t)
+            nc.vector.tensor_copy(b_sb[:], b_ps[t][:])
+            nc.vector.tensor_copy(pv[t % 3][:].indirect(idx3[:]), b_sb[:])
+
+        def gather_u(t):
+            u = keep.tile([P, O], F32, name="u%d" % t, tag="u%d" % t, align_bytes=64)
+            nc.scalar.activation(u[:], pw[t % 2][:].indirect(idx4[:]), ACT.Copy, scale=sa_t[:, t : t + 1])
+            us.append(u)
+
+        def gather_v(t):
+            v = keep.tile([P, O], F32, name="v%d" % t, tag="a_sb%d" % (t + 1) if t < PACK - 1 else "v_last", align_bytes=64)
+            nc.scalar.activation(v[:], pv[t % 3][:].indirect(idx5[:]), ACT.Copy, scale=sb_t[:, t : t + 1])
+            vs.append(v)
+
+        for t in (2, 3):
+            nc.vector.tensor_copy(a_sb[t][:], a_ps[t][:])
+        for t in range(3):
+            scatter_b(t)
+        scatter_a(0)
+        scatter_a(1)
+        gather_u(0)
+        gather_u(1)
+        gather_v(0)
+        scatter_b(3)
+        scatter_a(2)
+        gather_v(1)
+        scatter_a(3)
+        gather_u(2)
+        gather_v(2)
+        gather_u(3)
+        gather_v(3)
+
+        diff = keep.tile([P, PACK, O], F32, name="diff", tag="b_sb%d" % (PACK - 1))
+        for t in range(PACK):
+            nc.vector.tensor_tensor(diff[:, t, :], us[t][:], vs[t][:], ALU.subtract)
+
+        vss_g = keep.tile([P, N], U8, name="vss_g", tag="u0", align_bytes=64)
+        nc.vector.tensor_copy(vss_g[:], vss_win[:].indirect(idx6[:]))
+        vs_g = keep.tile([P, N], U16, name="vs_g", tag="v_last", align_bytes=64)
+        nc.vector.tensor_copy(vs_g[:], vs_win[:].indirect(idx6[:]))
+
+        hid = keep.tile([P, O, PACK], BF16, name="hid", align_bytes=64)
+        nc.scalar.activation(hid[:], diff[:].rearrange("p t o -> p o t"), ACT.Abs)
+        hid_codes = keep.tile([P, O], U32, name="hid_codes", align_bytes=64)
+        hid_scales = keep.tile([P, O], U8, name="hid_scales", align_bytes=64)
+        nc.vector.quantize_mx(
+            out=hid_codes[:].bitcast(E4M3X4), scales=hid_scales[:], in_=hid[:].rearrange("p o t -> p (o t)")
+        )
+
+        for h in range(N // P):
+            cols = slice(h * P, (h + 1) * P)
+            acc = psum.tile([P, O], F32, name="p%d" % h, tag="a%d" % h)
+            nc.tensor.matmul_mx(
+                out=acc[:], lhsT=vs_g[:, cols].bitcast(E2M1X4), lhsT_scale=vss_g[:, cols],
+                rhs=hid_codes[:].bitcast(E4M3X4), rhs_scale=hid_scales[:], start=True, stop=True,
+            )
+            p_sb = keep.tile([P, O], F32, name="p_sb%d" % h)
+            if h == 0:
+                nc.vector.tensor_copy(p_sb[:], acc[:])
+                nc.vector.tensor_copy(pages[h][:].indirect(idx7[:]), p_sb[:])
+                nc.sync.dma_start(out[cols, :], pages[h][:])
+            else:
+                nc.scalar.copy(p_sb[:], acc[:])
+                nc.scalar.activation(pages[h][:].indirect(idx7[:]), p_sb[:], ACT.Copy)
+                nc.scalar.dma_start(out[cols, :], pages[h][:])

@@ -30,6 +30,7 @@ def tile_list_owncommon_twow_store_scattered_kernel(
     nc = tc.nc
     with ExitStack() as ctx:
         keep = ctx.enter_context(tc.tile_pool(name="keep", bufs=1))
+        reuse = ctx.enter_context(tc.tile_pool(name="reuse", bufs=1))
         psum = ctx.enter_context(tc.psum_pool(name="psum", bufs=1))
 
         def load_list(name, src):
@@ -37,12 +38,10 @@ def tile_list_owncommon_twow_store_scattered_kernel(
             nc.sync.dma_start(tile[:], src)
             return tile
 
-        def load_scale_plane(name, scales, width):
-            window = keep.tile([P, width], U8, name=name, align_bytes=64)
-            nc.vector.memset(window[:].bitcast(I32), 0)
+        def load_scale_plane(window, engine, scales):
+            engine.memset(window[:].bitcast(I32), 0)
             for r in range(PACK):
                 nc.sync.dma_start(window[r:P:QUAD, :].bitcast(I32), scales[0, r : QUADS * PACK : PACK, :].bitcast(I32))
-            return window
 
         def load_scale_rows(name, scales):
             rows = keep.tile([PACK, QUADS, R], U8, name=name, align_bytes=64)
@@ -56,23 +55,25 @@ def tile_list_owncommon_twow_store_scattered_kernel(
                 nc.vector.tensor_copy(spread[QUAD * q : QUAD * q + PACK, :].bitcast(I32), rows[:, q, :].bitcast(I32))
             return spread
 
-        def deal_scales(name, spread):
-            dealt = keep.tile([P, R], U8, name=name + "_dealt", align_bytes=64)
+        def deal_scales(name, tag, spread):
+            dealt = keep.tile([P, R], U8, name=name + "_dealt", tag=tag, align_bytes=64)
             nc.vector.tensor_copy(
-                dealt[:].rearrange("p (t m) -> p m t", t=PACK), spread[:].rearrange("p (m t) -> p m t", t=PACK)
+                dealt[:].rearrange("p (t m) -> p t m", t=PACK), spread[:].rearrange("p (m t) -> p t m", t=PACK)
             )
             return dealt
 
         ws_rows = load_scale_rows("ws_rows", w_scales)
         idx = load_list("idx", offs)
-        xs_win = load_scale_plane("xs_win", xt_scales, T)
         w_raw = keep.tile([P, R], U16, name="w_raw", align_bytes=64)
         nc.sync.dma_start(w_raw[:].bitcast(I32), w_words[0].bitcast(I32))
-        xt_win = keep.tile([P, T], U32, name="xt_win", tag="page0", align_bytes=64)
+        xs_win = keep.tile([P, T], U8, name="xs_win", align_bytes=64)
+        load_scale_plane(xs_win, nc.vector, xt_scales)
+        xt_win = keep.tile([P, T], U32, name="xt_win", tag="xt_win", align_bytes=64)
         nc.sync.dma_start(xt_win[:].bitcast(I32), xt_words[0].rearrange("p n t -> p (n t)").bitcast(I32))
-        w2s_plane = load_scale_plane("w2s_plane", w2_scales, R)
-        w2_raw = keep.tile([P, R], U32, name="w2_raw", tag="page1", align_bytes=64)
+        w2_raw = keep.tile([P, R], U32, name="w2_raw", align_bytes=64)
         nc.sync.dma_start(w2_raw[:].bitcast(I32), w2_words[0].rearrange("p n t -> p (n t)").bitcast(I32))
+        w2s_plane = reuse.tile([P, R], U8, name="w2s_plane", offset=768, align_bytes=64)
+        load_scale_plane(w2s_plane, nc.vector, w2_scales)
         idx2 = load_list("idx2", offs2)
         idx3 = load_list("idx3", offs3)
         idx4 = load_list("idx4", offs4)
@@ -82,98 +83,104 @@ def tile_list_owncommon_twow_store_scattered_kernel(
         sb_t = keep.tile([P, PACK], F32, name="sb_t")
         nc.sync.dma_start(sb_t[:], sb.rearrange("(p t) o -> p (t o)", t=PACK))
 
-        ws = deal_scales("ws", spread_scales("ws", ws_rows))
+        ws = deal_scales("ws", "ws_dealt", spread_scales("ws", ws_rows))
         wd = keep.tile([P, R], U16, name="wd", align_bytes=64)
-        nc.scalar.copy(wd[:].rearrange("p (t m) -> p m t", t=PACK), w_raw[:].rearrange("p (m t) -> p m t", t=PACK))
-        xs_g = keep.tile([P, J], U8, name="xs_g", align_bytes=64)
+        nc.scalar.copy(wd[:].rearrange("p (t m) -> p t m", t=PACK), w_raw[:].rearrange("p (m t) -> p t m", t=PACK))
+        xs_g = keep.tile([P, J], U8, name="xs_g", tag="xs_g", align_bytes=64)
         nc.vector.tensor_copy(xs_g[:], xs_win[:].indirect(idx[:]))
-        x_g = keep.tile([P, J], U32, name="x_g", align_bytes=64)
+        x_g = keep.tile([P, J], U32, name="x_g", tag="x_g", align_bytes=64)
         nc.vector.tensor_copy(x_g[:], xt_win[:].indirect(idx[:]))
-        w2s = deal_scales("w2s", w2s_plane)
-        w2d = keep.tile([P, R], U32, name="w2d", align_bytes=64)
-        nc.vector.tensor_copy(
-            w2d[:].bitcast(I32).rearrange("p (t m) -> p m t", t=PACK),
-            w2_raw[:].bitcast(I32).rearrange("p (m t) -> p m t", t=PACK),
-        )
+        w2s = deal_scales("w2s", "xt_win", w2s_plane)
+        w2d = keep.tile([P, R], U32, name="w2d", tag="w2d", align_bytes=64)
+        nc.scalar.copy(w2d[:].rearrange("p (t m) -> p m t", t=PACK), w2_raw[:].rearrange("p (m t) -> p m t", t=PACK))
 
-        pw = [keep.tile([P, C], F32, name="pw%d" % i) for i in range(2)]
-        pv = [keep.tile([P, D], F32, name="pv%d" % i) for i in range(3)]
+        pw = [keep.tile([P, C], F32, name="pw%d" % i, tag="pw%d" % i, align_bytes=64) for i in range(2)]
+        pv = [keep.tile([P, D], F32, name="pv0")]
         for board in pw + pv:
             nc.vector.memset(board[:], 0.0)
 
         vs_win = keep.tile([P, S], U16, name="vs_win", align_bytes=64)
         nc.sync.dma_start(vs_win[:].bitcast(I32), vs_words[0].bitcast(I32))
         idx6 = load_list("idx6", offs6)
-        vss_win = load_scale_plane("vss_win", vs_scales, S)
         idx7 = load_list("idx7", offs7)
 
-        def product(name, words, scales, dtype, t):
-            acc = psum.tile([P, J], F32, name="%s%d" % (name, t), tag="%s%d" % (name, t))
+        def product(acc, words, scales, dtype, t):
             cols = slice(t * P, (t + 1) * P)
             nc.tensor.matmul_mx(
-                out=acc[:], lhsT=words[:, cols].bitcast(dtype), lhsT_scale=scales[:, cols],
+                out=acc, lhsT=words[:, cols].bitcast(dtype), lhsT_scale=scales[:, cols],
                 rhs=x_g[:].bitcast(E5M2X4), rhs_scale=xs_g[:], start=True, stop=True,
             )
-            return acc
 
-        a_ps = [product("a", wd, ws, E2M1X4, t) for t in range(PACK)]
-        b_ps = [product("b", w2d, w2s, E4M3X4, t) for t in range(PACK)]
+        a_ps = [psum.tile([P, J], F32, name="a%d" % t, tag="a%d" % t) for t in range(2)]
+        b_ps = [psum.tile([P, J], F32, name="b%d" % t) for t in range(2)]
+        a_ps_last = psum.tile([P, 2, J], F32, name="a_last")
+        b_ps_last = psum.tile([P, 2, J], F32, name="b_last")
+        product(a_ps[0][:], wd, ws, E2M1X4, 0)
+        product(a_ps[1][:], wd, ws, E2M1X4, 1)
+        product(b_ps[0][:], w2d, w2s, E4M3X4, 0)
+        for t in (2, 3):
+            product(a_ps_last[:, t - 2, :], wd, ws, E2M1X4, t)
+        product(b_ps[1][:], w2d, w2s, E4M3X4, 1)
+        for t in (2, 3):
+            product(b_ps_last[:, t - 2, :], w2d, w2s, E4M3X4, t)
 
-        pages = []
-        for h in range(N // P):
-            page = keep.tile([P, E], F32, name="page%d" % h, tag="page%d" % h, align_bytes=64)
-            for half in range(2):
-                nc.gpsimd.memset(page[:, half * (E // 2) : (half + 1) * (E // 2)], 0.0)
-            pages.append(page)
+        for i, tag in ((1, "xt_win"), (2, "w2d"), (3, "xs_g")):
+            board = keep.tile([P, D], F32, name="pv%d" % i, tag=tag, align_bytes=64)
+            nc.gpsimd.memset(board[:], 0.0)
+            pv.append(board)
+        vss_win = keep.tile([P, S], U8, name="vss_win", tag="x_g", align_bytes=64)
+        load_scale_plane(vss_win, nc.gpsimd, vs_scales)
 
-        a_sb = [keep.tile([P, J], F32, name="a_sb%d" % t, tag="a_sb%d" % t, align_bytes=64) for t in range(PACK)]
-        us, vs = [], []
+        a_sb0 = keep.tile([P, J], F32, name="a_sb0")
+        a_sb1 = reuse.tile([P, J], F32, name="a_sb1", offset=0, align_bytes=64)
+        a_sb_last = reuse.tile([P, 2, J], F32, name="a_sb_last", offset=1024, align_bytes=64)
+        a_sb = [a_sb0[:], a_sb1[:], a_sb_last[:, 0, :], a_sb_last[:, 1, :]]
+        b_sb0 = keep.tile([P, J], F32, name="b_sb0")
+        b_sb1 = keep.tile([P, J], F32, name="b_sb1", tag="b_sb1", align_bytes=64)
+        b_sb_last = reuse.tile([P, 2, J], F32, name="b_sb_last", offset=4096, align_bytes=64)
+        b_sb = [b_sb0[:], b_sb1[:], b_sb_last[:, 0, :], b_sb_last[:, 1, :]]
+        u = keep.tile([P, PACK, O], F32, name="u")
 
         def scatter_a(t):
-            if t < 2:
-                nc.scalar.copy(a_sb[t][:], a_ps[t][:])
-            nc.scalar.activation(pw[t % 2][:].indirect(idx2[:]), a_sb[t][:], ACT.Copy)
+            nc.scalar.activation(pw[t % 2][:].indirect(idx2[:]), a_sb[t], ACT.Copy)
 
         def scatter_b(t):
-            b_sb = keep.tile([P, J], F32, name="b_sb%d" % t, tag="b_sb%d" % t)
-            nc.vector.tensor_copy(b_sb[:], b_ps[t][:])
-            nc.vector.tensor_copy(pv[t % 3][:].indirect(idx3[:]), b_sb[:])
+            nc.vector.tensor_copy(pv[t][:].indirect(idx3[:]), b_sb[t])
 
         def gather_u(t):
-            u = keep.tile([P, O], F32, name="u%d" % t, tag="u%d" % t, align_bytes=64)
-            nc.scalar.activation(u[:], pw[t % 2][:].indirect(idx4[:]), ACT.Copy, scale=sa_t[:, t : t + 1])
-            us.append(u)
+            nc.scalar.activation(u[:, t, :], pw[t % 2][:].indirect(idx4[:]), ACT.Copy, scale=sa_t[:, t : t + 1])
 
-        def gather_v(t):
-            v = keep.tile([P, O], F32, name="v%d" % t, tag="a_sb%d" % (t + 1) if t < PACK - 1 else "v_last", align_bytes=64)
-            nc.scalar.activation(v[:], pv[t % 3][:].indirect(idx5[:]), ACT.Copy, scale=sb_t[:, t : t + 1])
-            vs.append(v)
-
-        for t in (2, 3):
-            nc.vector.tensor_copy(a_sb[t][:], a_ps[t][:])
-        for t in range(3):
-            scatter_b(t)
-        scatter_a(0)
-        scatter_a(1)
-        gather_u(0)
-        gather_u(1)
-        gather_v(0)
+        nc.scalar.copy(a_sb[0], a_ps[0][:])
+        nc.vector.tensor_copy(a_sb[1], a_ps[1][:])
+        nc.vector.tensor_copy(b_sb[0], b_ps[0][:])
+        scatter_b(0)
+        nc.vector.tensor_copy(a_sb_last[:], a_ps_last[:])
+        nc.vector.tensor_copy(b_sb[1], b_ps[1][:])
+        scatter_b(1)
+        nc.vector.tensor_copy(b_sb_last[:], b_ps_last[:])
+        scatter_b(2)
         scatter_b(3)
-        scatter_a(2)
-        gather_v(1)
-        scatter_a(3)
-        gather_u(2)
-        gather_v(2)
-        gather_u(3)
-        gather_v(3)
-
-        diff = keep.tile([P, PACK, O], F32, name="diff", tag="b_sb%d" % (PACK - 1))
+        for t0 in (0, 2):
+            scatter_a(t0)
+            scatter_a(t0 + 1)
+            gather_u(t0)
+            gather_u(t0 + 1)
+        v = reuse.tile([P, PACK, O], F32, name="v", offset=2048, align_bytes=64)
         for t in range(PACK):
-            nc.vector.tensor_tensor(diff[:, t, :], us[t][:], vs[t][:], ALU.subtract)
+            nc.scalar.activation(v[:, t, :], pv[t][:].indirect(idx5[:]), ACT.Copy, scale=sb_t[:, t : t + 1])
 
-        vss_g = keep.tile([P, N], U8, name="vss_g", tag="u0", align_bytes=64)
+        pages = []
+        for h, tag in enumerate(("b_sb1", "pw0")):
+            page = keep.tile([P, E], F32, name="page%d" % h, tag=tag, align_bytes=64)
+            nc.gpsimd.memset(page[:], 0.0)
+            pages.append(page)
+
+        vss_g = reuse.tile([P, N], U8, name="vss_g", offset=4096, align_bytes=64)
         nc.vector.tensor_copy(vss_g[:], vss_win[:].indirect(idx6[:]))
-        vs_g = keep.tile([P, N], U16, name="vs_g", tag="v_last", align_bytes=64)
+        diff = keep.tile([P, PACK, O], F32, name="diff", tag="x_g", align_bytes=64)
+        for planes in (slice(0, PACK - 1), slice(PACK - 1, PACK)):
+            nc.vector.tensor_tensor(diff[:, planes, :], u[:, planes, :], v[:, planes, :], ALU.subtract)
+        vs_g = reuse.tile([P, N], U16, name="vs_g", offset=2048, align_bytes=64)
         nc.vector.tensor_copy(vs_g[:], vs_win[:].indirect(idx6[:]))
 
         hid = keep.tile([P, O, PACK], BF16, name="hid", align_bytes=64)

from contextlib import ExitStack

import concourse.mybir as mybir

K, T, J, R, C, D, O, N, S, E = 512, 1024, 256, 512, 512, 512, 128, 256, 1024, 1024
FLOPS = 2 * K * R * J * 2 + 2 * R * N * O

F32 = mybir.dt.float32
BF16 = mybir.dt.bfloat16
I32 = mybir.dt.int32
U32 = mybir.dt.uint32
U16 = mybir.dt.uint16
U8 = mybir.dt.uint8
E4M3X4 = mybir.dt.float8_e4m3fn_x4
E5M2X4 = mybir.dt.float8_e5m2_x4
E2M1X4 = mybir.dt.float4_e2m1fn_x4
ACT = mybir.ActivationFunctionType
ALU = mybir.AluOpType

P = 128
PACK = 4
QUADS = 4
QUAD = 32


def tile_list_owncommon_twow_store_scattered_kernel(
    tc, xt_words, xt_scales, w_words, w_scales, w2_words, w2_scales, sa, sb, vs_words, vs_scales,
    offs, offs2, offs3, offs4, offs5, offs6, offs7, out,
):
    nc = tc.nc
    with ExitStack() as ctx:
        keep = ctx.enter_context(tc.tile_pool(name="keep", bufs=1))
        reuse = ctx.enter_context(tc.tile_pool(name="reuse", bufs=1))
        psum = ctx.enter_context(tc.psum_pool(name="psum", bufs=1))

        def load_list(name, src):
            tile = keep.tile(list(src.shape), U16, name=name)
            nc.sync.dma_start(tile[:], src)
            return tile

        def load_scale_plane(window, engine, scales):
            engine.memset(window[:].bitcast(I32), 0)
            for r in range(PACK):
                nc.sync.dma_start(window[r:P:QUAD, :].bitcast(I32), scales[0, r : QUADS * PACK : PACK, :].bitcast(I32))

        def load_scale_rows(name, scales):
            rows = keep.tile([PACK, QUADS, R], U8, name=name, align_bytes=64)
            nc.sync.dma_start(rows[:].bitcast(I32), scales[0].rearrange("(q r) n -> r q n", r=PACK).bitcast(I32))
            return rows

        def spread_scales(name, rows):
            spread = keep.tile([P, R], U8, name=name + "_spread", align_bytes=64)
            nc.vector.memset(spread[:].bitcast(I32), 0)
            for q in range(QUADS):
                nc.vector.tensor_copy(spread[QUAD * q : QUAD * q + PACK, :].bitcast(I32), rows[:, q, :].bitcast(I32))
            return spread

        def deal_scales(name, tag, spread):
            dealt = keep.tile([P, R], U8, name=name + "_dealt", tag=tag, align_bytes=64)
            nc.vector.tensor_copy(
                dealt[:].rearrange("p (t m) -> p t m", t=PACK), spread[:].rearrange("p (m t) -> p t m", t=PACK)
            )
            return dealt

        ws_rows = load_scale_rows("ws_rows", w_scales)
        idx = load_list("idx", offs)
        w_raw = keep.tile([P, R], U16, name="w_raw", align_bytes=64)
        nc.sync.dma_start(w_raw[:].bitcast(I32), w_words[0].bitcast(I32))
        xs_win = keep.tile([P, T], U8, name="xs_win", align_bytes=64)
        load_scale_plane(xs_win, nc.vector, xt_scales)
        xt_win = keep.tile([P, T], U32, name="xt_win", tag="xt_win", align_bytes=64)
        nc.sync.dma_start(xt_win[:].bitcast(I32), xt_words[0].rearrange("p n t -> p (n t)").bitcast(I32))
        w2_raw = keep.tile([P, R], U32, name="w2_raw", align_bytes=64)
        nc.sync.dma_start(w2_raw[:].bitcast(I32), w2_words[0].rearrange("p n t -> p (n t)").bitcast(I32))
        w2s_plane = reuse.tile([P, R], U8, name="w2s_plane", offset=768, align_bytes=64)
        load_scale_plane(w2s_plane, nc.vector, w2_scales)
        idx2 = load_list("idx2", offs2)
        idx3 = load_list("idx3", offs3)
        idx4 = load_list("idx4", offs4)
        sa_t = keep.tile([P, PACK], F32, name="sa_t")
        nc.sync.dma_start(sa_t[:], sa.rearrange("(p t) o -> p (t o)", t=PACK))
        idx5 = load_list("idx5", offs5)
        sb_t = keep.tile([P, PACK], F32, name="sb_t")
        nc.sync.dma_start(sb_t[:], sb.rearrange("(p t) o -> p (t o)", t=PACK))

        ws = deal_scales("ws", "ws_dealt", spread_scales("ws", ws_rows))
        wd = keep.tile([P, R], U16, name="wd", align_bytes=64)
        nc.scalar.copy(wd[:].rearrange("p (t m) -> p t m", t=PACK), w_raw[:].rearrange("p (m t) -> p t m", t=PACK))
        xs_g = keep.tile([P, J], U8, name="xs_g", tag="xs_g", align_bytes=64)
        nc.vector.tensor_copy(xs_g[:], xs_win[:].indirect(idx[:]))
        x_g = keep.tile([P, J], U32, name="x_g", tag="x_g", align_bytes=64)
        nc.vector.tensor_copy(x_g[:], xt_win[:].indirect(idx[:]))
        w2s = deal_scales("w2s", "xt_win", w2s_plane)
        w2d = keep.tile([P, R], U32, name="w2d", tag="w2d", align_bytes=64)
        nc.scalar.copy(w2d[:].rearrange("p (t m) -> p m t", t=PACK), w2_raw[:].rearrange("p (m t) -> p m t", t=PACK))

        pw = [keep.tile([P, C], F32, name="pw%d" % i, tag="pw%d" % i, align_bytes=64) for i in range(2)]
        pv = [keep.tile([P, D], F32, name="pv0")]
        for board in pw + pv:
            nc.vector.memset(board[:], 0.0)

        vs_win = keep.tile([P, S], U16, name="vs_win", align_bytes=64)
        nc.sync.dma_start(vs_win[:].bitcast(I32), vs_words[0].bitcast(I32))
        idx6 = load_list("idx6", offs6)
        idx7 = load_list("idx7", offs7)

        def product(acc, words, scales, dtype, t):
            cols = slice(t * P, (t + 1) * P)
            nc.tensor.matmul_mx(
                out=acc, lhsT=words[:, cols].bitcast(dtype), lhsT_scale=scales[:, cols],
                rhs=x_g[:].bitcast(E5M2X4), rhs_scale=xs_g[:], start=True, stop=True,
            )

        a_ps = [psum.tile([P, J], F32, name="a%d" % t, tag="a%d" % t) for t in range(2)]
        b_ps = [psum.tile([P, J], F32, name="b%d" % t) for t in range(2)]
        a_ps_last = psum.tile([P, 2, J], F32, name="a_last")
        b_ps_last = psum.tile([P, 2, J], F32, name="b_last")
        product(a_ps[0][:], wd, ws, E2M1X4, 0)
        product(a_ps[1][:], wd, ws, E2M1X4, 1)
        product(b_ps[0][:], w2d, w2s, E4M3X4, 0)
        for t in (2, 3):
            product(a_ps_last[:, t - 2, :], wd, ws, E2M1X4, t)
        product(b_ps[1][:], w2d, w2s, E4M3X4, 1)
        for t in (2, 3):
            product(b_ps_last[:, t - 2, :], w2d, w2s, E4M3X4, t)

        for i, tag in ((1, "xt_win"), (2, "w2d"), (3, "xs_g")):
            board = keep.tile([P, D], F32, name="pv%d" % i, tag=tag, align_bytes=64)
            nc.gpsimd.memset(board[:], 0.0)
            pv.append(board)
        vss_win = keep.tile([P, S], U8, name="vss_win", tag="x_g", align_bytes=64)
        load_scale_plane(vss_win, nc.gpsimd, vs_scales)

        a_sb0 = keep.tile([P, J], F32, name="a_sb0")
        a_sb1 = reuse.tile([P, J], F32, name="a_sb1", offset=0, align_bytes=64)
        a_sb_last = reuse.tile([P, 2, J], F32, name="a_sb_last", offset=1024, align_bytes=64)
        a_sb = [a_sb0[:], a_sb1[:], a_sb_last[:, 0, :], a_sb_last[:, 1, :]]
        b_sb0 = keep.tile([P, J], F32, name="b_sb0")
        b_sb1 = keep.tile([P, J], F32, name="b_sb1", tag="b_sb1", align_bytes=64)
        b_sb_last = reuse.tile([P, 2, J], F32, name="b_sb_last", offset=4096, align_bytes=64)
        b_sb = [b_sb0[:], b_sb1[:], b_sb_last[:, 0, :], b_sb_last[:, 1, :]]
        u = keep.tile([P, PACK, O], F32, name="u")

        def scatter_a(t):
            nc.scalar.activation(pw[t % 2][:].indirect(idx2[:]), a_sb[t], ACT.Copy)

        def scatter_b(t):
            nc.vector.tensor_copy(pv[t][:].indirect(idx3[:]), b_sb[t])

        def gather_u(t):
            nc.scalar.activation(u[:, t, :], pw[t % 2][:].indirect(idx4[:]), ACT.Copy, scale=sa_t[:, t : t + 1])

        nc.scalar.copy(a_sb[0], a_ps[0][:])
        nc.vector.tensor_copy(a_sb[1], a_ps[1][:])
        nc.vector.tensor_copy(b_sb[0], b_ps[0][:])
        scatter_b(0)
        nc.vector.tensor_copy(a_sb_last[:], a_ps_last[:])
        nc.vector.tensor_copy(b_sb[1], b_ps[1][:])
        scatter_b(1)
        nc.vector.tensor_copy(b_sb_last[:], b_ps_last[:])
        scatter_b(2)
        scatter_b(3)
        for t0 in (0, 2):
            scatter_a(t0)
            scatter_a(t0 + 1)
            gather_u(t0)
            gather_u(t0 + 1)
        v = reuse.tile([P, PACK, O], F32, name="v", offset=2048, align_bytes=64)
        for t in range(PACK):
            nc.scalar.activation(v[:, t, :], pv[t][:].indirect(idx5[:]), ACT.Copy, scale=sb_t[:, t : t + 1])

        pages = []
        for h, tag in enumerate(("b_sb1", "pw0")):
            page = keep.tile([P, E], F32, name="page%d" % h, tag=tag, align_bytes=64)
            nc.gpsimd.memset(page[:], 0.0)
            pages.append(page)

        vss_g = reuse.tile([P, N], U8, name="vss_g", offset=4096, align_bytes=64)
        nc.vector.tensor_copy(vss_g[:], vss_win[:].indirect(idx6[:]))
        diff = keep.tile([P, PACK, O], F32, name="diff", tag="x_g", align_bytes=64)
        for planes in (slice(0, PACK - 1), slice(PACK - 1, PACK)):
            nc.vector.tensor_tensor(diff[:, planes, :], u[:, planes, :], v[:, planes, :], ALU.subtract)
        vs_g = reuse.tile([P, N], U16, name="vs_g", offset=2048, align_bytes=64)
        nc.vector.tensor_copy(vs_g[:], vs_win[:].indirect(idx6[:]))

        hid = keep.tile([P, O, PACK], BF16, name="hid", align_bytes=64)
        nc.scalar.activation(hid[:], diff[:].rearrange("p t o -> p o t"), ACT.Abs)
        hid_codes = keep.tile([P, O], U32, name="hid_codes", align_bytes=64)
        hid_scales = keep.tile([P, O], U8, name="hid_scales", align_bytes=64)
        nc.vector.quantize_mx(
            out=hid_codes[:].bitcast(E4M3X4), scales=hid_scales[:], in_=hid[:].rearrange("p o t -> p (o t)")
        )

        for h in range(N // P):
            cols = slice(h * P, (h + 1) * P)
            acc = psum.tile([P, O], F32, name="p%d" % h, tag="a%d" % h)
            nc.tensor.matmul_mx(
                out=acc[:], lhsT=vs_g[:, cols].bitcast(E2M1X4), lhsT_scale=vss_g[:, cols],
                rhs=hid_codes[:].bitcast(E4M3X4), rhs_scale=hid_scales[:], start=True, stop=True,
            )
            p_sb = keep.tile([P, O], F32, name="p_sb%d" % h)
            if h == 0:
                nc.vector.tensor_copy(p_sb[:], acc[:])
                nc.vector.tensor_copy(pages[h][:].indirect(idx7[:]), p_sb[:])
                nc.sync.dma_start(out[cols, :], pages[h][:])
            else:
                nc.scalar.copy(p_sb[:], acc[:])
                nc.scalar.activation(pages[h][:].indirect(idx7[:]), p_sb[:], ACT.Copy)
                nc.scalar.dma_start(out[cols, :], pages[h][:])
